import numpy as np, ml_dtypes
CORES = [24,25,26,27,28,29,30,31]
N = 8
BF = ml_dtypes.bfloat16
def gentries(a):
    return np.ascontiguousarray(a.reshape(8, 16, -1).transpose(0, 2, 1)).reshape(8, -1)
def gtable(e):
    e = np.asarray(e); return np.ascontiguousarray(e.reshape(8, -1, 16).transpose(0, 2, 1)).reshape(128, -1).astype(np.int32)
V, R = 2048, 4
def family(rng, sizes, depth, pool, mix, fall=None):
    key = np.tile(np.arange(V), (N, 1)); lev = np.zeros(V, np.int64); comp = np.zeros(V, np.int64); via = [-1] * V; o = rng.permutation(V); a = 0
    for i in range(len(sizes)):
        s, D = int(sizes[i]), int(depth[i]); m = o[a:a + s]; a += s; comp[m] = i
        if s == 1: continue
        root = int(np.min(m)); m = m[m != root]; l = np.concatenate([np.arange(1, D + 1), rng.integers(1, D + 1, s - 1 - D)])
        if fall is not None and fall[i]: m = np.sort(m)[::-1]; l = np.sort(l)
        lev[m] = l
        at = [[root]] + [[] for k in range(D)]
        for c, k in zip(m.tolist(), l.tolist()): at[k].append(c)
        for k in range(1, D + 1):
            for c in at[k]:
                p = at[k - 1][int(rng.integers(len(at[k - 1])))]; w = [q for q in pool if q != via[p]]; q = w[int(rng.integers(len(w)))]
                key[q, c] = key[q, p]; via[c] = q
    for q in range(N if mix > 0 else 0):
        h = np.flatnonzero(key[q] == np.arange(V)); t = comp[h] * (R + 1) + lev[h]; keep = rng.random(h.size) >= mix
        hk, tk = h[keep], t[keep]; s = np.argsort(tk, kind="stable"); hk, tk = hk[s], tk[s]
        lo = np.searchsorted(tk, t, "left"); n = np.searchsorted(tk, t, "right") - lo; z = ~keep & (n > 0)
        to = h + 0; to[z] = hk[lo[z] + (rng.random(np.count_nonzero(z)) * n[z]).astype(np.int64)]
        jump = np.arange(V); jump[h] = to; key[q] = jump[key[q]]
    return key
def lay(rng, key, way):
    if way == 0: o = np.lexsort((rng.random(V), rng.permutation(V)[key]))
    elif way == 1: o = np.lexsort((np.arange(V), key))
    else: o = np.lexsort((-np.arange(V), -key))
    k = key[o]; s = np.ones(V, np.int64); s[1:] = k[1:] != k[:-1]
    e = np.append(np.flatnonzero(s)[1:], V) - 1; last = np.zeros(V, np.int64); last[o] = e[np.add.accumulate(s) - 1]
    return [o, s, last]
def pack(rng, keys, ways):
    a = np.array([[lay(rng, keys[g][q], ways[q, g]) for g in range(8)] for q in range(N)])
    return {"pm": np.stack([gtable(u) for u in a[:, :, 0]]), "en": np.stack([gtable(u) for u in a[:, :, 2]]), "st": np.ascontiguousarray(a[:, :, 1]).astype(np.int32)}
def depths(rng, s):
    top = np.minimum(R, s - 1); D = np.where(top > 0, 1 + (rng.random(s.size) * top).astype(np.int64), 0); i = np.argmax(s); D[i] = top[i]; return D
def some(rng):
    out = []
    for n in rng.choice(np.arange(6, 41), 8, replace=False):
        c = np.sort(rng.choice(V - 1, int(n) - 1, replace=False)) + 1; s = np.diff(np.concatenate([[0], c, [V]]))
        out.append(family(rng, s, depths(rng, s), list(range(N)), rng.choice([0.0, 0.05, 0.15])))
    return out
def setup_inputs(rng):
    return pack(rng, some(rng), np.zeros((N, 8), np.int64))
def setup_inputs_deep(rng):
    few = rng.permutation(8)[:4]; n = rng.choice(np.arange(V // (2 * (R + 1)), V // (R + 1) + 1), 8, replace=False); keys = []
    for g in range(8):
        m = int(n[g]); s = [R + 1] * m + [1] * (V - m * (R + 1)); pool = rng.permutation(N)[:2].tolist() if g in few else list(range(N))
        keys.append(family(rng, s, [R] * m + [0] * (V - m * (R + 1)), pool, 0.0, np.arange(len(s)) % 2 == 0))
    return pack(rng, keys, np.zeros((N, 8), np.int64))
def setup_inputs_ends(rng):
    keys = some(rng); w = rng.permutation(8); one = np.tile(np.arange(V), (N, 1))
    keys[w[0]][rng.integers(N)] = 0
    keys[w[1]] = one + 0
    keys[w[2]] = np.tile(rng.integers(0, 30, V), (N, 1))
    keys[w[3]] = one + 0; keys[w[3]][rng.integers(N)] = rng.integers(0, 3, V)
    x = np.concatenate([[0], 1 + rng.choice(V - 2, R - 1, replace=False), [V - 1]]); k = one + 0; ab = rng.permutation(N)[:2]
    for i in range(R): k[ab[i % 2], x[i + 1]] = x[i]
    keys[w[4]] = k
    return pack(rng, keys, np.zeros((N, 8), np.int64))
def setup_inputs_order(rng):
    return pack(rng, some(rng), rng.integers(1, 3, (N, 8)))
def setup_inputs_spread(rng):
    keys = []; half = int(rng.integers(8))
    for g in range(8):
        s = [1] * (V // 2 if g == half else 0); left = V - len(s)
        while left > 0:
            t = max(1, int(left * (0.3 + 0.4 * rng.random()))); s.append(t); left -= t
        s = np.array(s); keys.append(family(rng, s, depths(rng, s), list(range(N)) + [int(rng.integers(N))] * (3 * N), rng.choice([0.0, 0.3, 0.8])))
    return pack(rng, keys, np.zeros((N, 8), np.int64))
def hop(p, st, L):
    g = np.arange(8)[:, None]; M = L
    for q in range(N):
        s = st[q].reshape(-1); m = np.minimum.reduceat(L[g, p[q]].reshape(-1), np.flatnonzero(s))
        u = np.empty_like(L); u[g, p[q]] = m[np.add.accumulate(s) - 1].reshape(8, V); M = np.minimum(M, u)
    return M
def check_inputs(d):
    p = np.stack([gentries(a) for a in d["pm"]]); e = np.stack([gentries(a) for a in d["en"]]); s = d["st"]
    if not (np.sort(p, -1) == np.arange(V)).all(): return ["pm: every vertex once"]
    if not (((s == 0) | (s == 1)).all() and (s[:, :, 0] == 1).all()): return ["st: 0 and 1, beginning with 1"]
    bad = []; t = s.reshape(-1); last = ((np.append(np.flatnonzero(t)[1:], t.size) - 1) % V)[np.add.accumulate(t) - 1].reshape(N, 8, V)
    if not (np.take_along_axis(e, p, 2) == last).all(): bad.append("en: last places")
    L = np.tile(np.arange(V), (8, 1))
    for i in range(R): L = hop(p, s, L)
    if not (hop(p, s, L) == L).all(): bad.append("at most R steps to the smallest vertex")
    return bad
def reference(pm, en, st):
    p = np.stack([gentries(a) for a in pm]); L = np.tile(np.arange(V), (8, 1))
    while True:
        M = hop(p, st, L)
        if (M == L).all(): break
        L = M
    c = np.count_nonzero(L == np.arange(V), axis=1).reshape(8, 1)
    return {"y": np.stack([L for r in range(N)]).astype(np.float32), "cnt": np.stack([c for r in range(N)]).astype(np.float32)}

@@ -1,0 +1,245 @@
+import math
+from concourse.bass import DstId, RemoteDMATransfer
+from concourse.mybir import AluOpType as A, AxisListType, ActivationFunctionType as F
+
+BF, F32, I32, U16 = "bfloat16", "float32", "int32", "uint16"
+V = 2048
+SCRATCH = {
+    "dtx": ("dram", [8, 128, 32], I32), "drx": ("dram", [8, 128, 32], I32),
+    "dst": ("dram", [8, 128, 16], BF), "drs": ("dram", [8, 128, 16], BF),
+    "pmi": ("sbuf", [128, 128], I32), "eni": ("sbuf", [128, 128], I32),
+    "pmo": ("sbuf", [128, 128], U16), "eno": ("sbuf", [128, 128], U16),
+    "pmi2": ("sbuf", [128, 128], I32), "eni2": ("sbuf", [128, 128], I32),
+    "pmo2": ("sbuf", [128, 128], U16), "eno2": ("sbuf", [128, 128], U16),
+    "stm": ("sbuf", [128, V], BF), "stm2": ("sbuf", [128, V], BF),
+    "win": ("sbuf", [128, V], BF), "plc": ("sbuf", [128, V], BF),
+    "cls": ("sbuf", [128, V], BF), "ver": ("sbuf", [128, V], BF),
+    "red": ("sbuf", [128, 128], BF), "rows": ("sbuf", [128, 128], BF),
+    "xs": ("sbuf", [128, 128], BF), "land": ("sbuf", [128, 128], BF),
+    "t64": ("sbuf", [128, 64], BF), "t32": ("sbuf", [128, 32], BF), "t16": ("sbuf", [128, 16], BF),
+    "ys": ("sbuf", [128, 16], BF), "land2": ("sbuf", [128, 128], BF),
+    "flg": ("sbuf", [128, 128], BF), "lnv": ("sbuf", [128, 128], F32),
+    "yi": ("sbuf", [128, 128], I32), "yf": ("sbuf", [128, 128], F32), "cf": ("sbuf", [128, 4], F32),
+    "ones": ("sbuf", [128, 128], BF), "ident": ("sbuf", [128, 128], BF), "sel": ("sbuf", [128, 8], BF),
+    "selb": ("sbuf", [128, V], BF), "msk": ("sbuf", [128, 128], BF), "ratio": ("sbuf", [128, 128], F32),
+    "enc": ("sbuf", [128, 128], BF), "c2": ("sbuf", [128, 4], F32), "lnc": ("sbuf", [128, 4], F32),
+    "acol": ("sbuf", [128, 4], F32),
+    "psA": ("psum", [128, 512], F32), "psB": ("psum", [128, 512], F32), "psC": ("psum", [128, 512], F32),
+    "psD": ("psum", [128, 512], F32), "psE": ("psum", [128, 512], F32), "psX": ("psum", [128, 512], F32),
+    "psR": ("psum", [128, 512], F32), "psT": ("psum", [128, 512], F32),
+}
+SEMAPHORES = ("dpm den dtx down dlist dmask dy dcnt gd1 gd2 arrL arrS arrM arrY loc vones gident gsel vstm vc2 sac "
+              "vrt vw0 vw1 vw2 vw3 vpm ven pe0 venc vmsk vselb szero vp2 vg sg0 sg1 sg2 sc0 sc1 sc2 sc3 "
+              "vm0 vm1 sm0 sm1 px vxs vown vt1 vt2 vred pr vrow pwA pwB pwC pwD pwE wv ws vys vown2 pt sln vyi vyf "
+              "vflg pc scf").split()
+
+X0, X1, X2 = 704, 1216, 1728
+BANKS = [("A", 0, 256), ("B", 256, 512), ("C", 768, 512), ("D", 1280, 512), ("E", 1792, 256)]
+
+
+def rank_program(g, core, T, topo):
+    me = T.rank_of(core)
+    if me is None:
+        return
+    ve, se, pe, sy = g.vector, g.scalar, g.tensor, g.sync
+    n = {s: 0 for s in SEMAPHORES}
+
+    def inc(ins, name, k=1):
+        ins.then_inc(T.sem[name], k)
+        n[name] += k
+
+    def wait(queue, *names):
+        for s in names:
+            queue.wait_ge(T.sem[s], n[s])
+
+    others = [c for c in T.cores if c != core]
+    far = [c for c in others if topo.die(c) != topo.die(core)]
+    near = [c for c in others if topo.die(c) == topo.die(core)]
+    order = []
+    while far or near:
+        if far:
+            order.append(far.pop(0))
+        if near:
+            order.append(near.pop(0))
+
+    def send(src_of, dst, arr):
+        trs = []
+        for k, c in enumerate(order):
+            e = topo.engines(core, c)
+            m = (1 << e[k]) | (1 << e[k + len(e) // 2])
+            rid, pid, _s = topo.addr(c)
+            trs.append(RemoteDMATransfer(dst_ids=[DstId(rid=rid, pnc=pid)], dma_engine_mask=m, remote_sem=T.sem[arr],
+                                         src=src_of(T.rank_of(c)), dst=dst))
+            n["loc"] += 2
+            n[arr] += 2
+        g.remote_dma_fused(trs, local_sem=T.sem.loc)
+
+    inc(sy.dma_start(T.pmi[:], T.pm[:]), "dpm", 16)
+    inc(se.dma_start(T.eni[:], T.en[:]), "den", 16)
+    inc(sy.dma_start(T.dtx[:, 0:64, :], T.pm[:]), "dtx", 16)
+    inc(se.dma_start(T.dtx[:, 64:128, :], T.en[:]), "dtx", 16)
+    own = slice(16 * me, 16 * me + 16)
+    inc(sy.dma_start(T.drx[me, 0:64, :], T.pm[own, :]), "down", 16)
+    inc(sy.dma_start(T.drx[me, 64:128, :], T.en[own, :]), "down", 16)
+
+    inc(ve.memset(T.ones[:], 1.0), "vones")
+    inc(ve.memset(T.stm[:], 0.0), "vstm")
+    inc(ve.memset(T.c2[:, 0:2], math.exp(16.0 / math.log(2.0))), "vc2")
+    inc(ve.memset(T.ratio[:], 2.0 ** (1.0 / 32)), "vrt")
+
+    wait(g, "vones")
+    inc(g.affine_select(T.ident[:], T.ones[:], [[-1, 128]], A.is_equal, 0.0, 0, 1), "gident")
+    inc(g.affine_select(T.sel[:], T.ones[:, 0:8], [[-16, 8]], A.is_equal, 0.0, 0, 1), "gsel")
+    wait(g, "vstm")
+    inc(g.dma_start(T.stm[0:128:16, :], T.st[:]), "gd1", 16)
+    inc(g.dma_start(T.dst[:], T.st[:]), "gd2", 16)
+
+    wait(se, "vc2")
+    inc(se.activation(T.lnc[:, 0:2], T.c2[:, 0:2], F.Ln, accum_out=T.acol[:, 0:1]), "sac")
+
+    wait(ve, "vrt")
+    inc(ve.tensor_tensor_scan(T.win[:, 0:128], T.ratio[:], T.ratio[:], 2.0 ** (-64 - 1.0 / 32), A.mult, A.min), "vw0")
+    wait(ve, "vw0")
+    inc(ve.tensor_scalar(T.win[:, 128:256], T.win[:, 0:128], 2.0 ** 4, None, A.mult), "vw1")
+    wait(ve, "vw1")
+    inc(ve.tensor_scalar(T.win[:, 256:512], T.win[:, 0:256], 2.0 ** 8, None, A.mult), "vw2")
+    wait(ve, "vw2")
+    for k in (1, 2, 3):
+        inc(ve.tensor_scalar(T.win[:, 512 * k:512 * k + 512], T.win[:, 0:512], 2.0 ** (16 * k), None, A.mult), "vw3")
+    wait(ve, "dpm")
+    inc(ve.tensor_copy(T.pmo[:], T.pmi[:]), "vpm")
+
+    wait(g, "dtx")
+    send(lambda r: T.dtx[r], T.drx[me], "arrL")
+    wait(g, "gd2")
+    send(lambda r: T.dst[r], T.drs[me], "arrS")
+    wait(sy, "gd2")
+    inc(sy.dma_start(T.drs[me], T.dst[me]), "down", 16)
+    wait(sy, "down", "arrL")
+    inc(sy.dma_start(T.pmi2[:], T.drx[:, 0:64, :]), "dlist", 16)
+    inc(sy.dma_start(T.eni2[:], T.drx[:, 64:128, :]), "dlist", 16)
+
+    wait(pe, "vw3", "vw2", "gsel")
+    for b in range(16):
+        inc(pe.matmul(T.psT[:, b:128:16], T.win[:, 128 * b:128 * b + 128], T.sel[:], True, True), "pe0")
+
+    def phase(first, pmo, eno, stm, ready, turn):
+        wait(ve, *ready)
+        inc(ve.tensor_copy(T.plc[:, 0:X0], T.win[:].indirect(pmo[:, 0:X0 // 16])), "vg")
+        wait(se, *ready)
+        cut = [X0, X1, X2, V]
+        for k in range(3):
+            a, b = cut[k], cut[k + 1]
+            inc(se.activation(T.plc[:, a:b], T.win[:].indirect(pmo[:, a // 16:b // 16]), F.Copy), "sg%d" % k)
+        if first:
+            wait(ve, "den")
+            inc(ve.tensor_copy(T.eno[:], T.eni[:]), "ven")
+            wait(ve, "gd1")
+        else:
+            wait(ve, "dmask")
+        lo = 0
+        for k, hi in enumerate(cut):
+            wait(ve, "vg" if k == 0 else "sg%d" % (k - 1))
+            if k:
+                wait(ve, "sc%d" % (k - 1))
+            inc(ve.tensor_tensor_scan(T.cls[:, lo:hi], stm[:, lo:hi], T.plc[:, lo:hi],
+                                      T.cls[:, lo - 1:lo] if k else 1.0, A.max, A.min), "sc%d" % k)
+            lo = hi
+        wait(ve, "sc3")
+        wait(se, "sc3")
+        if first:
+            wait(ve, "ven")
+            wait(se, "ven")
+        for k in range(2):
+            a = 512 * k
+            inc(ve.tensor_copy(T.ver[:, a:a + 512], T.cls[:].indirect(eno[:, a // 16:a // 16 + 32])), "vm%d" % k)
+            a = 1024 + 512 * k
+            inc(se.activation(T.ver[:, a:a + 512], T.cls[:].indirect(eno[:, a // 16:a // 16 + 32]), F.Copy), "sm%d" % k)
+        for s, b0 in (("vm0", 0), ("sm0", 8), ("vm1", 4), ("sm1", 12)):
+            wait(pe, s)
+            for b in range(b0, b0 + 4):
+                inc(pe.matmul(turn(b), T.ver[:, 128 * b:128 * b + 128], T.sel[:], True, True), "px")
+
+    phase(True, T.pmo, T.eno, T.stm, ("vw3", "vw2", "vpm"), lambda b: T.psX[:, b:128:16])
+    inc(se.activation(T.stm2[:], T.stm[:], F.Copy, scale=0.0), "szero")
+    wait(sy, "szero", "arrS")
+    inc(sy.dma_start(T.stm2[0:128:16, :], T.drs[:]), "dmask", 16)
+    wait(ve, "px")
+    inc(ve.tensor_copy(T.xs[:], T.psX[:, 0:128]), "vxs")
+    wait(g, "vxs")
+    send(lambda r: T.xs[:, 16 * r:16 * r + 16], T.land[:, 16 * me:16 * me + 16], "arrM")
+    mine = slice(16 * me, 16 * me + 16)
+    wait(ve, "vxs")
+    inc(ve.tensor_copy(T.land[:, mine], T.xs[:, mine]), "vown")
+    wait(ve, "gident")
+    for b in range(16):
+        inc(ve.tensor_scalar(T.selb[0:16, 128 * b:128 * b + 128], T.ones[0:16, :], T.ident[0:16, b:b + 1], None, A.mult),
+            "vselb")
+    wait(ve, "dlist")
+    inc(ve.tensor_copy(T.pmo2[:], T.pmi2[:]), "vp2")
+    inc(ve.tensor_copy(T.eno2[:], T.eni2[:]), "vp2")
+    inc(ve.memset(T.msk[:], 0.0), "vmsk")
+    wait(ve, "vmsk")
+    inc(ve.memset(T.msk[:, 0:128:8], 1.0), "vmsk")
+    wait(ve, "pe0")
+    inc(ve.tensor_copy(T.enc[:], T.psT[:, 0:128]), "venc")
+    wait(ve, "arrM", "vown")
+    inc(ve.tensor_tensor(T.t64[:], T.land[:, 0:64], T.land[:, 64:128], A.min), "vt1")
+    wait(ve, "vt1")
+    inc(ve.tensor_tensor(T.t32[:], T.t64[:, 0:32], T.t64[:, 32:64], A.min), "vt2")
+    wait(ve, "vt2")
+    inc(ve.tensor_tensor(T.t16[:], T.t32[:, 0:16], T.t32[:, 16:32], A.min), "vred")
+    lab = T.t16[:]
+
+    for h in (2, 3, 4):
+        wait(pe, "vred", "gident", "vselb")
+        inc(pe.matmul(T.psR[0:16, 0:128], lab, T.ident[:], True, True), "pr")
+        wait(ve, "pr")
+        inc(ve.tensor_copy(T.rows[0:16, :], T.psR[0:16, 0:128]), "vrow")
+        wait(pe, "vrow")
+        for name, c0, w in BANKS:
+            for j in range(w // 128):
+                b = c0 // 128 + j
+                inc(pe.matmul(T["ps" + name][:, 128 * j:128 * j + 128], T.selb[0:16, 128 * b:128 * b + 128],
+                              T.rows[0:16, :], True, True), "pw" + name)
+        for name, c0, w in BANKS:
+            if name in "ACE":
+                wait(ve, "pw" + name)
+                inc(ve.tensor_copy(T.win[:, c0:c0 + w], T["ps" + name][:, 0:w]), "wv")
+            else:
+                wait(se, "pw" + name)
+                inc(se.activation(T.win[:, c0:c0 + w], T["ps" + name][:, 0:w], F.Copy), "ws")
+        phase(False, T.pmo2, T.eno2, T.stm2, ("wv", "ws", "vp2"), lambda b: T.psX[:, 8 * b:8 * b + 8])
+        wait(ve, "px", "vmsk")
+        inc(ve.tensor_tensor_scan(T.red[:], T.msk[:], T.psX[:, 0:128], 1.0, A.max, A.min), "vred")
+        lab = T.red[:, 7:128:8]
+
+    wait(ve, "vred")
+    inc(ve.tensor_copy(T.ys[:], lab), "vys")
+    wait(g, "vys")
+    send(lambda r: T.ys[:], T.land2[:, mine], "arrY")
+    wait(ve, "vys")
+    inc(ve.tensor_copy(T.land2[:, mine], T.ys[:]), "vown2")
+    wait(pe, "arrY", "vown2")
+    inc(pe.matmul(T.psT[:, 0:128], T.land2[:], T.ident[:], True, True), "pt")
+    wait(ve, "arrY", "vown2", "venc")
+    inc(ve.tensor_tensor(T.flg[:], T.land2[:], T.enc[:], A.is_equal), "vflg")
+    wait(se, "pt")
+    inc(se.activation(T.lnv[:], T.psT[:, 0:128], F.Ln, scale=2.0 ** 32), "sln")
+    wait(ve, "sln", "sac")
+    inc(ve.tensor_scalar(T.yi[:], T.lnv[:], T.acol[:, 0:1], 1024.0, A.mult, A.add), "vyi")
+    wait(ve, "vyi")
+    inc(ve.tensor_copy(T.yf[:], T.yi[:]), "vyf")
+    wait(sy, "vyf")
+    inc(sy.dma_start(T.y[:], T.yf[:]), "dy", 16)
+    wait(pe, "vflg", "vones")
+    for b in range(16):
+        pc = pe.matmul(T.psR[0:8, 0:1], T.flg[:, b:128:16], T.ones[:, 0:1], b == 0, b == 15)
+    inc(pc, "pc")
+    wait(se, "pc")
+    inc(se.activation(T.cf[0:8, 0:1], T.psR[0:8, 0:1], F.Copy), "scf")
+    wait(se, "scf")
+    inc(se.dma_start(T.cnt[:], T.cf[0:8, 0:1]), "dcnt", 16)
+    wait(sy, "dy")
+    wait(se, "dcnt")
+    wait(g, "loc", "gd1", "gd2")

@@ -14,27 +14,31 @@ SCRATCH = {
     "stm": ("sbuf", [128, V], BF), "stm2": ("sbuf", [128, V], BF),
     "win": ("sbuf", [128, V], BF), "plc": ("sbuf", [128, V], BF),
     "cls": ("sbuf", [128, V], BF), "ver": ("sbuf", [128, V], BF),
-    "red": ("sbuf", [128, 128], BF), "rows": ("sbuf", [128, 128], BF),
+    "red": ("sbuf", [128, 256], BF), "per": ("sbuf", [128, 144], BF),
     "xs": ("sbuf", [128, 128], BF), "land": ("sbuf", [128, 128], BF),
-    "t64": ("sbuf", [128, 64], BF), "t32": ("sbuf", [128, 32], BF), "t16": ("sbuf", [128, 16], BF),
+    "t64": ("sbuf", [128, 64], BF), "t32": ("sbuf", [128, 32], BF),
     "ys": ("sbuf", [128, 16], BF), "land2": ("sbuf", [128, 128], BF),
     "flg": ("sbuf", [128, 128], BF), "lnv": ("sbuf", [128, 128], F32),
     "yi": ("sbuf", [128, 128], I32), "yf": ("sbuf", [128, 128], F32), "cf": ("sbuf", [128, 4], F32),
     "ones": ("sbuf", [128, 128], BF), "ident": ("sbuf", [128, 128], BF), "sel": ("sbuf", [128, 8], BF),
-    "selb": ("sbuf", [128, V], BF), "msk": ("sbuf", [128, 128], BF), "ratio": ("sbuf", [128, 128], F32),
+    "sel2": ("sbuf", [128, 16], BF), "msk": ("sbuf", [128, 256], BF), "ratio": ("sbuf", [128, 128], F32),
     "enc": ("sbuf", [128, 128], BF), "c2": ("sbuf", [128, 4], F32), "lnc": ("sbuf", [128, 4], F32),
-    "acol": ("sbuf", [128, 4], F32),
-    "psA": ("psum", [128, 512], F32), "psB": ("psum", [128, 512], F32), "psC": ("psum", [128, 512], F32),
-    "psD": ("psum", [128, 512], F32), "psE": ("psum", [128, 512], F32), "psX": ("psum", [128, 512], F32),
+    "acol": ("sbuf", [128, 4], F32), "hal": ("sbuf", [128, 4], F32), "big": ("sbuf", [128, 4], F32),
+    "bigb": ("sbuf", [128, 4], BF),
+    "pi": ("sbuf", [128, 10], I32), "pa": ("sbuf", [128, 10], I32), "pb": ("sbuf", [128, 10], I32),
+    "pc8": ("sbuf", [128, 10], I32), "pd": ("sbuf", [128, 10], I32), "pe16": ("sbuf", [128, 10], I32),
+    "pl": ("sbuf", [128, 10], U16),
+    "psA": ("psum", [128, 1024], BF), "psB": ("psum", [128, 1024], BF), "psC": ("psum", [128, 1024], BF),
+    "psD": ("psum", [128, 1024], BF), "psE": ("psum", [128, 1024], BF), "psX": ("psum", [128, 512], F32),
     "psR": ("psum", [128, 512], F32), "psT": ("psum", [128, 512], F32),
 }
-SEMAPHORES = ("dpm den dtx down dlist dmask dy dcnt gd1 gd2 arrL arrS arrM arrY loc vones gident gsel vstm vc2 sac "
-              "vrt vw0 vw1 vw2 vw3 vpm ven pe0 venc vmsk vselb szero vp2 vg sg0 sg1 sg2 sc0 sc1 sc2 sc3 "
-              "vm0 vm1 sm0 sm1 px vxs vown vt1 vt2 vred pr vrow pwA pwB pwC pwD pwE wv ws vys vown2 pt sln vyi vyf "
-              "vflg pc scf").split()
+SEMAPHORES = ("dpm den dtx down dlist dmask dy dcnt gd1 gd2 arrL arrS arrM arrY loc vones gident gsel gpi vstm vc2 sac "
+              "vrt vw0 vw1 vw2 vw3 sw3 vpm ven pe0 venc vmsk vrd0 vhal vbig vp1 vp3 vp4 vp5 szero vp2 vg sg0 sg1 sg2 sc0 "
+              "sc1 sc2 sc3 vm0 vm1 sm0 sm1 px vxs vown vt1 vt2 vred vper sper pwA pwB pwC pwD pwE wv ws vys vown2 pt sln "
+              "vyi vyf vflg pc scf").split()
 
 X0, X1, X2 = 704, 1216, 1728
-BANKS = [("A", 0, 256), ("B", 256, 512), ("C", 768, 512), ("D", 1280, 512), ("E", 1792, 256)]
+BANKS = [("B", 0, 1), ("A", 1, 1), ("D", 2, 2), ("C", 4, 2), ("E", 6, 2)]
 
 
 def rank_program(g, core, T, topo):
@@ -82,9 +86,9 @@ def rank_program(g, core, T, topo):
     inc(sy.dma_start(T.drx[me, 0:64, :], T.pm[own, :]), "down", 16)
     inc(sy.dma_start(T.drx[me, 64:128, :], T.en[own, :]), "down", 16)
 
+    inc(ve.memset(T.c2[:, 0:2], math.exp(16.0 / math.log(2.0))), "vc2")
     inc(ve.memset(T.ones[:], 1.0), "vones")
     inc(ve.memset(T.stm[:], 0.0), "vstm")
-    inc(ve.memset(T.c2[:, 0:2], math.exp(16.0 / math.log(2.0))), "vc2")
     inc(ve.memset(T.ratio[:], 2.0 ** (1.0 / 32)), "vrt")
 
     wait(g, "vones")
@@ -93,6 +97,8 @@ def rank_program(g, core, T, topo):
     wait(g, "vstm")
     inc(g.dma_start(T.stm[0:128:16, :], T.st[:]), "gd1", 16)
     inc(g.dma_start(T.dst[:], T.st[:]), "gd2", 16)
+    inc(g.affine_select(T.sel2[:], T.ones[:, 0:16], [[-16, 8], [-1, 2]], A.is_equal, 0.0, 0, 1), "gsel")
+    inc(g.iota(T.pi[:], [[0, 10]], 0, 1), "gpi")
 
     wait(se, "vc2")
     inc(se.activation(T.lnc[:, 0:2], T.c2[:, 0:2], F.Ln, accum_out=T.acol[:, 0:1]), "sac")
@@ -103,8 +109,10 @@ def rank_program(g, core, T, topo):
     inc(ve.tensor_scalar(T.win[:, 128:256], T.win[:, 0:128], 2.0 ** 4, None, A.mult), "vw1")
     wait(ve, "vw1")
     inc(ve.tensor_scalar(T.win[:, 256:512], T.win[:, 0:256], 2.0 ** 8, None, A.mult), "vw2")
+    wait(se, "vw2")
+    inc(se.activation(T.win[:, 1536:2048], T.win[:, 0:512], F.Copy, scale=2.0 ** 48), "sw3")
     wait(ve, "vw2")
-    for k in (1, 2, 3):
+    for k in (1, 2):
         inc(ve.tensor_scalar(T.win[:, 512 * k:512 * k + 512], T.win[:, 0:512], 2.0 ** (16 * k), None, A.mult), "vw3")
     wait(ve, "dpm")
     inc(ve.tensor_copy(T.pmo[:], T.pmi[:]), "vpm")
@@ -119,11 +127,11 @@ def rank_program(g, core, T, topo):
     inc(sy.dma_start(T.pmi2[:], T.drx[:, 0:64, :]), "dlist", 16)
     inc(sy.dma_start(T.eni2[:], T.drx[:, 64:128, :]), "dlist", 16)
 
-    wait(pe, "vw3", "vw2", "gsel")
+    wait(pe, "vw3", "vw2", "sw3", "gsel")
     for b in range(16):
         inc(pe.matmul(T.psT[:, b:128:16], T.win[:, 128 * b:128 * b + 128], T.sel[:], True, True), "pe0")
 
-    def phase(first, pmo, eno, stm, ready, turn):
+    def phase(first, pmo, eno, stm, ready, turn, sel):
         wait(ve, *ready)
         inc(ve.tensor_copy(T.plc[:, 0:X0], T.win[:].indirect(pmo[:, 0:X0 // 16])), "vg")
         wait(se, *ready)
@@ -150,72 +158,87 @@ def rank_program(g, core, T, topo):
         if first:
             wait(ve, "ven")
             wait(se, "ven")
-        for k in range(2):
-            a = 512 * k
-            inc(ve.tensor_copy(T.ver[:, a:a + 512], T.cls[:].indirect(eno[:, a // 16:a // 16 + 32])), "vm%d" % k)
-            a = 1024 + 512 * k
-            inc(se.activation(T.ver[:, a:a + 512], T.cls[:].indirect(eno[:, a // 16:a // 16 + 32]), F.Copy), "sm%d" % k)
-        for s, b0 in (("vm0", 0), ("sm0", 8), ("vm1", 4), ("sm1", 12)):
+        for k, a, b in ((0, 0, 768), (1, 768, 1024)):
+            inc(ve.tensor_copy(T.ver[:, a:b], T.cls[:].indirect(eno[:, a // 16:b // 16])), "vm%d" % k)
+            a, b = a + 1024, b + 1024
+            inc(se.activation(T.ver[:, a:b], T.cls[:].indirect(eno[:, a // 16:b // 16]), F.Copy), "sm%d" % k)
+        for s, b0, b1 in (("vm0", 0, 6), ("sm0", 8, 14), ("vm1", 6, 8), ("sm1", 14, 16)):
             wait(pe, s)
-            for b in range(b0, b0 + 4):
-                inc(pe.matmul(turn(b), T.ver[:, 128 * b:128 * b + 128], T.sel[:], True, True), "px")
+            for b in range(b0, b1):
+                inc(pe.matmul(turn(b), T.ver[:, 128 * b:128 * b + 128], sel, True, True), "px")
 
-    phase(True, T.pmo, T.eno, T.stm, ("vw3", "vw2", "vpm"), lambda b: T.psX[:, b:128:16])
+    phase(True, T.pmo, T.eno, T.stm, ("vw3", "vw2", "sw3", "vpm"), lambda b: T.psX[:, b:128:16], T.sel[:])
     inc(se.activation(T.stm2[:], T.stm[:], F.Copy, scale=0.0), "szero")
-    wait(sy, "szero", "arrS")
-    inc(sy.dma_start(T.stm2[0:128:16, :], T.drs[:]), "dmask", 16)
+    wait(sy, "szero", "arrS", "down")
+    for k in (0, 1):
+        inc(sy.dma_start(T.stm2[k:128:16, :], T.drs[0:8]), "dmask", 16)
     wait(ve, "px")
     inc(ve.tensor_copy(T.xs[:], T.psX[:, 0:128]), "vxs")
     wait(g, "vxs")
-    send(lambda r: T.xs[:, 16 * r:16 * r + 16], T.land[:, 16 * me:16 * me + 16], "arrM")
     mine = slice(16 * me, 16 * me + 16)
+    send(lambda r: T.xs[:, 16 * r:16 * r + 16], T.land[:, mine], "arrM")
     wait(ve, "vxs")
     inc(ve.tensor_copy(T.land[:, mine], T.xs[:, mine]), "vown")
-    wait(ve, "gident")
-    for b in range(16):
-        inc(ve.tensor_scalar(T.selb[0:16, 128 * b:128 * b + 128], T.ones[0:16, :], T.ident[0:16, b:b + 1], None, A.mult),
-            "vselb")
+    inc(ve.memset(T.msk[:], 0.0), "vmsk")
+    inc(ve.memset(T.red[:], 1.0), "vrd0")
+    wait(ve, "vmsk")
+    inc(ve.memset(T.msk[:, 0:256:16], 1.0), "vmsk")
+    wait(ve, "gsel")
+    for k in (0, 1):
+        inc(ve.tensor_reduce(T.hal[:, k:k + 1], T.sel2[:, k:16:2], AxisListType.X, A.max), "vhal")
+    wait(ve, "vhal")
+    inc(ve.tensor_scalar(T.big[:, 0:2], T.hal[:, 0:2], -1.0, 1.0, A.mult, A.add), "vbig")
+    inc(ve.tensor_scalar(T.bigb[:, 0:2], T.hal[:, 0:2], -1.0, 1.0, A.mult, A.add), "vbig")
+    wait(ve, "gpi")
+    inc(ve.tensor_scalar(T.pa[:], T.pi[:], 14, None, A.bitwise_and), "vp1")
+    inc(ve.tensor_scalar(T.pb[:], T.pi[:], 1, None, A.bitwise_and), "vp1")
+    wait(ve, "vp1")
+    inc(ve.tensor_scalar(T.pc8[:], T.pa[:], 8, 15, A.mult, A.add), "vp3")
+    inc(ve.tensor_scalar(T.pd[:], T.pb[:], 128, None, A.mult), "vp3")
+    wait(ve, "vp3")
+    inc(ve.tensor_tensor(T.pe16[:], T.pc8[:], T.pd[:], A.add), "vp4")
+    wait(ve, "vp4")
+    inc(ve.tensor_copy(T.pl[:], T.pe16[:]), "vp5")
     wait(ve, "dlist")
     inc(ve.tensor_copy(T.pmo2[:], T.pmi2[:]), "vp2")
     inc(ve.tensor_copy(T.eno2[:], T.eni2[:]), "vp2")
-    inc(ve.memset(T.msk[:], 0.0), "vmsk")
-    wait(ve, "vmsk")
-    inc(ve.memset(T.msk[:, 0:128:8], 1.0), "vmsk")
     wait(ve, "pe0")
     inc(ve.tensor_copy(T.enc[:], T.psT[:, 0:128]), "venc")
     wait(ve, "arrM", "vown")
     inc(ve.tensor_tensor(T.t64[:], T.land[:, 0:64], T.land[:, 64:128], A.min), "vt1")
     wait(ve, "vt1")
     inc(ve.tensor_tensor(T.t32[:], T.t64[:, 0:32], T.t64[:, 32:64], A.min), "vt2")
-    wait(ve, "vt2")
-    inc(ve.tensor_tensor(T.t16[:], T.t32[:, 0:16], T.t32[:, 16:32], A.min), "vred")
-    lab = T.t16[:]
+    wait(ve, "vt2", "vrd0")
+    inc(ve.tensor_tensor(T.red[:, 15:256:16], T.t32[:, 0:16], T.t32[:, 16:32], A.min), "vred")
 
     for h in (2, 3, 4):
-        wait(pe, "vred", "gident", "vselb")
-        inc(pe.matmul(T.psR[0:16, 0:128], lab, T.ident[:], True, True), "pr")
-        wait(ve, "pr")
-        inc(ve.tensor_copy(T.rows[0:16, :], T.psR[0:16, 0:128]), "vrow")
-        wait(pe, "vrow")
-        for name, c0, w in BANKS:
-            for j in range(w // 128):
-                b = c0 // 128 + j
-                inc(pe.matmul(T["ps" + name][:, 128 * j:128 * j + 128], T.selb[0:16, 128 * b:128 * b + 128],
-                              T.rows[0:16, :], True, True), "pw" + name)
-        for name, c0, w in BANKS:
-            if name in "ACE":
-                wait(ve, "pw" + name)
-                inc(ve.tensor_copy(T.win[:, c0:c0 + w], T["ps" + name][:, 0:w]), "wv")
-            else:
-                wait(se, "pw" + name)
-                inc(se.activation(T.win[:, c0:c0 + w], T["ps" + name][:, 0:w], F.Copy), "ws")
-        phase(False, T.pmo2, T.eno2, T.stm2, ("wv", "ws", "vp2"), lambda b: T.psX[:, 8 * b:8 * b + 8])
+        wait(ve, "vred", "vp5")
+        inc(ve.tensor_copy(T.per[:, 0:96], T.red[:].indirect(T.pl[:, 0:6])), "vper")
+        wait(se, "vred", "vp5")
+        inc(se.activation(T.per[:, 96:144], T.red[:].indirect(T.pl[:, 6:9]), F.Copy), "sper")
+        wait(pe, "vper", "sper", "gident")
+        for name, b0, k in BANKS:
+            for j in range(k):
+                b = b0 + j
+                inc(pe.transpose(T["ps" + name][:, 128 * j:128 * j + 128], T.per[:, 2 * b:2 * b + 128], T.ident[:]),
+                    "pw" + name)
+        for name, b0, k in BANKS:
+            src, lo, hi = T["ps" + name][:, 0:128 * k], 128 * b0, 128 * (b0 + k)
+            for half in (0, 1):
+                dst = T.win[:, 1024 * half + lo:1024 * half + hi]
+                if name in "ACE":
+                    wait(ve, "pw" + name, "vbig")
+                    inc(ve.tensor_scalar(dst, src, T.bigb[:, half:half + 1], None, A.max), "wv")
+                else:
+                    wait(se, "pw" + name, "vbig")
+                    inc(se.activation(dst, src, F.Identity, bias=T.big[:, half:half + 1],
+                                      scale=T.hal[:, half:half + 1]), "ws")
+        phase(False, T.pmo2, T.eno2, T.stm2, ("wv", "ws", "vp2"), lambda b: T.psX[:, 16 * b:16 * b + 16], T.sel2[:])
         wait(ve, "px", "vmsk")
-        inc(ve.tensor_tensor_scan(T.red[:], T.msk[:], T.psX[:, 0:128], 1.0, A.max, A.min), "vred")
-        lab = T.red[:, 7:128:8]
+        inc(ve.tensor_tensor_scan(T.red[:], T.msk[:], T.psX[:, 0:256], 1.0, A.max, A.min), "vred")
 
     wait(ve, "vred")
-    inc(ve.tensor_copy(T.ys[:], lab), "vys")
+    inc(ve.tensor_copy(T.ys[:], T.red[:, 15:256:16]), "vys")
     wait(g, "vys")
     send(lambda r: T.ys[:], T.land2[:, mine], "arrY")
     wait(ve, "vys")
@@ -242,4 +265,4 @@ def rank_program(g, core, T, topo):
     inc(se.dma_start(T.cnt[:], T.cf[0:8, 0:1]), "dcnt", 16)
     wait(sy, "dy")
     wait(se, "dcnt")
-    wait(g, "loc", "gd1", "gd2")
+    wait(g, "loc")

import math
from concourse.bass import DstId, RemoteDMATransfer
from concourse.mybir import AluOpType as A, AxisListType, ActivationFunctionType as F

BF, F32, I32, U16 = "bfloat16", "float32", "int32", "uint16"
V = 2048
SCRATCH = {
    "dtx": ("dram", [8, 128, 32], I32), "drx": ("dram", [8, 128, 32], I32),
    "dst": ("dram", [8, 128, 16], BF), "drs": ("dram", [8, 128, 16], BF),
    "pmi": ("sbuf", [128, 128], I32), "eni": ("sbuf", [128, 128], I32),
    "pmo": ("sbuf", [128, 128], U16), "eno": ("sbuf", [128, 128], U16),
    "pmi2": ("sbuf", [128, 128], I32), "eni2": ("sbuf", [128, 128], I32),
    "pmo2": ("sbuf", [128, 128], U16), "eno2": ("sbuf", [128, 128], U16),
    "stm": ("sbuf", [128, V], BF), "stm2": ("sbuf", [128, V], BF),
    "win": ("sbuf", [128, V], BF), "plc": ("sbuf", [128, V], BF),
    "cls": ("sbuf", [128, V], BF), "ver": ("sbuf", [128, V], BF),
    "red": ("sbuf", [128, 256], BF), "per": ("sbuf", [128, 144], BF),
    "xs": ("sbuf", [128, 128], BF), "land": ("sbuf", [128, 128], BF),
    "t64": ("sbuf", [128, 64], BF), "t32": ("sbuf", [128, 32], BF),
    "ys": ("sbuf", [128, 16], BF), "land2": ("sbuf", [128, 128], BF),
    "flg": ("sbuf", [128, 128], BF), "lnv": ("sbuf", [128, 128], F32),
    "yi": ("sbuf", [128, 128], I32), "yf": ("sbuf", [128, 128], F32), "cf": ("sbuf", [128, 4], F32),
    "ones": ("sbuf", [128, 128], BF), "ident": ("sbuf", [128, 128], BF), "sel": ("sbuf", [128, 8], BF),
    "sel2": ("sbuf", [128, 16], BF), "msk": ("sbuf", [128, 256], BF), "ratio": ("sbuf", [128, 128], F32),
    "enc": ("sbuf", [128, 128], BF), "c2": ("sbuf", [128, 4], F32), "lnc": ("sbuf", [128, 4], F32),
    "acol": ("sbuf", [128, 4], F32), "hal": ("sbuf", [128, 4], F32), "big": ("sbuf", [128, 4], F32),
    "bigb": ("sbuf", [128, 4], BF),
    "pi": ("sbuf", [128, 10], I32), "pa": ("sbuf", [128, 10], I32), "pb": ("sbuf", [128, 10], I32),
    "pc8": ("sbuf", [128, 10], I32), "pd": ("sbuf", [128, 10], I32), "pe16": ("sbuf", [128, 10], I32),
    "pl": ("sbuf", [128, 10], U16),
    "psA": ("psum", [128, 1024], BF), "psB": ("psum", [128, 1024], BF), "psC": ("psum", [128, 1024], BF),
    "psD": ("psum", [128, 1024], BF), "psE": ("psum", [128, 1024], BF), "psX": ("psum", [128, 512], F32),
    "psR": ("psum", [128, 512], F32), "psT": ("psum", [128, 512], F32),
}
SEMAPHORES = ("dpm den dtx down dlist dmask dy dcnt gd1 gd2 arrL arrS arrM arrY loc vones gident gsel gpi vstm vc2 sac "
              "vrt vw0 vw1 vw2 vw3 sw3 vpm ven pe0 venc vmsk vrd0 vhal vbig vp1 vp3 vp4 vp5 szero vp2 vg sg0 sg1 sg2 sc0 "
              "sc1 sc2 sc3 vm0 vm1 sm0 sm1 px vxs vown vt1 vt2 vred vper sper pwA pwB pwC pwD pwE wv ws vys vown2 pt sln "
              "vyi vyf vflg pc scf").split()

X0, X1, X2 = 704, 1216, 1728
BANKS = [("B", 0, 1), ("A", 1, 1), ("D", 2, 2), ("C", 4, 2), ("E", 6, 2)]


def rank_program(g, core, T, topo):
    me = T.rank_of(core)
    if me is None:
        return
    ve, se, pe, sy = g.vector, g.scalar, g.tensor, g.sync
    n = {s: 0 for s in SEMAPHORES}

    def inc(ins, name, k=1):
        ins.then_inc(T.sem[name], k)
        n[name] += k

    def wait(queue, *names):
        for s in names:
            queue.wait_ge(T.sem[s], n[s])

    others = [c for c in T.cores if c != core]
    far = [c for c in others if topo.die(c) != topo.die(core)]
    near = [c for c in others if topo.die(c) == topo.die(core)]
    order = []
    while far or near:
        if far:
            order.append(far.pop(0))
        if near:
            order.append(near.pop(0))

    def send(src_of, dst, arr):
        trs = []
        for k, c in enumerate(order):
            e = topo.engines(core, c)
            m = (1 << e[k]) | (1 << e[k + len(e) // 2])
            rid, pid, _s = topo.addr(c)
            trs.append(RemoteDMATransfer(dst_ids=[DstId(rid=rid, pnc=pid)], dma_engine_mask=m, remote_sem=T.sem[arr],
                                         src=src_of(T.rank_of(c)), dst=dst))
            n["loc"] += 2
            n[arr] += 2
        g.remote_dma_fused(trs, local_sem=T.sem.loc)

    inc(sy.dma_start(T.pmi[:], T.pm[:]), "dpm", 16)
    inc(se.dma_start(T.eni[:], T.en[:]), "den", 16)
    inc(sy.dma_start(T.dtx[:, 0:64, :], T.pm[:]), "dtx", 16)
    inc(se.dma_start(T.dtx[:, 64:128, :], T.en[:]), "dtx", 16)
    own = slice(16 * me, 16 * me + 16)
    inc(sy.dma_start(T.drx[me, 0:64, :], T.pm[own, :]), "down", 16)
    inc(sy.dma_start(T.drx[me, 64:128, :], T.en[own, :]), "down", 16)

    inc(ve.memset(T.c2[:, 0:2], math.exp(16.0 / math.log(2.0))), "vc2")
    inc(ve.memset(T.ones[:], 1.0), "vones")
    inc(ve.memset(T.stm[:], 0.0), "vstm")
    inc(ve.memset(T.ratio[:], 2.0 ** (1.0 / 32)), "vrt")

    wait(g, "vones")
    inc(g.affine_select(T.ident[:], T.ones[:], [[-1, 128]], A.is_equal, 0.0, 0, 1), "gident")
    inc(g.affine_select(T.sel[:], T.ones[:, 0:8], [[-16, 8]], A.is_equal, 0.0, 0, 1), "gsel")
    wait(g, "vstm")
    inc(g.dma_start(T.stm[0:128:16, :], T.st[:]), "gd1", 16)
    inc(g.dma_start(T.dst[:], T.st[:]), "gd2", 16)
    inc(g.affine_select(T.sel2[:], T.ones[:, 0:16], [[-16, 8], [-1, 2]], A.is_equal, 0.0, 0, 1), "gsel")
    inc(g.iota(T.pi[:], [[0, 10]], 0, 1), "gpi")

    wait(se, "vc2")
    inc(se.activation(T.lnc[:, 0:2], T.c2[:, 0:2], F.Ln, accum_out=T.acol[:, 0:1]), "sac")

    wait(ve, "vrt")
    inc(ve.tensor_tensor_scan(T.win[:, 0:128], T.ratio[:], T.ratio[:], 2.0 ** (-64 - 1.0 / 32), A.mult, A.min), "vw0")
    wait(ve, "vw0")
    inc(ve.tensor_scalar(T.win[:, 128:256], T.win[:, 0:128], 2.0 ** 4, None, A.mult), "vw1")
    wait(ve, "vw1")
    inc(ve.tensor_scalar(T.win[:, 256:512], T.win[:, 0:256], 2.0 ** 8, None, A.mult), "vw2")
    wait(se, "vw2")
    inc(se.activation(T.win[:, 1536:2048], T.win[:, 0:512], F.Copy, scale=2.0 ** 48), "sw3")
    wait(ve, "vw2")
    for k in (1, 2):
        inc(ve.tensor_scalar(T.win[:, 512 * k:512 * k + 512], T.win[:, 0:512], 2.0 ** (16 * k), None, A.mult), "vw3")
    wait(ve, "dpm")
    inc(ve.tensor_copy(T.pmo[:], T.pmi[:]), "vpm")

    wait(g, "dtx")
    send(lambda r: T.dtx[r], T.drx[me], "arrL")
    wait(g, "gd2")
    send(lambda r: T.dst[r], T.drs[me], "arrS")
    wait(sy, "gd2")
    inc(sy.dma_start(T.drs[me], T.dst[me]), "down", 16)
    wait(sy, "down", "arrL")
    inc(sy.dma_start(T.pmi2[:], T.drx[:, 0:64, :]), "dlist", 16)
    inc(sy.dma_start(T.eni2[:], T.drx[:, 64:128, :]), "dlist", 16)

    wait(pe, "vw3", "vw2", "sw3", "gsel")
    for b in range(16):
        inc(pe.matmul(T.psT[:, b:128:16], T.win[:, 128 * b:128 * b + 128], T.sel[:], True, True), "pe0")

    def phase(first, pmo, eno, stm, ready, turn, sel):
        wait(ve, *ready)
        inc(ve.tensor_copy(T.plc[:, 0:X0], T.win[:].indirect(pmo[:, 0:X0 // 16])), "vg")
        wait(se, *ready)
        cut = [X0, X1, X2, V]
        for k in range(3):
            a, b = cut[k], cut[k + 1]
            inc(se.activation(T.plc[:, a:b], T.win[:].indirect(pmo[:, a // 16:b // 16]), F.Copy), "sg%d" % k)
        if first:
            wait(ve, "den")
            inc(ve.tensor_copy(T.eno[:], T.eni[:]), "ven")
            wait(ve, "gd1")
        else:
            wait(ve, "dmask")
        lo = 0
        for k, hi in enumerate(cut):
            wait(ve, "vg" if k == 0 else "sg%d" % (k - 1))
            if k:
                wait(ve, "sc%d" % (k - 1))
            inc(ve.tensor_tensor_scan(T.cls[:, lo:hi], stm[:, lo:hi], T.plc[:, lo:hi],
                                      T.cls[:, lo - 1:lo] if k else 1.0, A.max, A.min), "sc%d" % k)
            lo = hi
        wait(ve, "sc3")
        wait(se, "sc3")
        if first:
            wait(ve, "ven")
            wait(se, "ven")
        for k, a, b in ((0, 0, 768), (1, 768, 1024)):
            inc(ve.tensor_copy(T.ver[:, a:b], T.cls[:].indirect(eno[:, a // 16:b // 16])), "vm%d" % k)
            a, b = a + 1024, b + 1024
            inc(se.activation(T.ver[:, a:b], T.cls[:].indirect(eno[:, a // 16:b // 16]), F.Copy), "sm%d" % k)
        for s, b0, b1 in (("vm0", 0, 6), ("sm0", 8, 14), ("vm1", 6, 8), ("sm1", 14, 16)):
            wait(pe, s)
            for b in range(b0, b1):
                inc(pe.matmul(turn(b), T.ver[:, 128 * b:128 * b + 128], sel, True, True), "px")

    phase(True, T.pmo, T.eno, T.stm, ("vw3", "vw2", "sw3", "vpm"), lambda b: T.psX[:, b:128:16], T.sel[:])
    inc(se.activation(T.stm2[:], T.stm[:], F.Copy, scale=0.0), "szero")
    wait(sy, "szero", "arrS", "down")
    for k in (0, 1):
        inc(sy.dma_start(T.stm2[k:128:16, :], T.drs[0:8]), "dmask", 16)
    wait(ve, "px")
    inc(ve.tensor_copy(T.xs[:], T.psX[:, 0:128]), "vxs")
    wait(g, "vxs")
    mine = slice(16 * me, 16 * me + 16)
    send(lambda r: T.xs[:, 16 * r:16 * r + 16], T.land[:, mine], "arrM")
    wait(ve, "vxs")
    inc(ve.tensor_copy(T.land[:, mine], T.xs[:, mine]), "vown")
    inc(ve.memset(T.msk[:], 0.0), "vmsk")
    inc(ve.memset(T.red[:], 1.0), "vrd0")
    wait(ve, "vmsk")
    inc(ve.memset(T.msk[:, 0:256:16], 1.0), "vmsk")
    wait(ve, "gsel")
    for k in (0, 1):
        inc(ve.tensor_reduce(T.hal[:, k:k + 1], T.sel2[:, k:16:2], AxisListType.X, A.max), "vhal")
    wait(ve, "vhal")
    inc(ve.tensor_scalar(T.big[:, 0:2], T.hal[:, 0:2], -1.0, 1.0, A.mult, A.add), "vbig")
    inc(ve.tensor_scalar(T.bigb[:, 0:2], T.hal[:, 0:2], -1.0, 1.0, A.mult, A.add), "vbig")
    wait(ve, "gpi")
    inc(ve.tensor_scalar(T.pa[:], T.pi[:], 14, None, A.bitwise_and), "vp1")
    inc(ve.tensor_scalar(T.pb[:], T.pi[:], 1, None, A.bitwise_and), "vp1")
    wait(ve, "vp1")
    inc(ve.tensor_scalar(T.pc8[:], T.pa[:], 8, 15, A.mult, A.add), "vp3")
    inc(ve.tensor_scalar(T.pd[:], T.pb[:], 128, None, A.mult), "vp3")
    wait(ve, "vp3")
    inc(ve.tensor_tensor(T.pe16[:], T.pc8[:], T.pd[:], A.add), "vp4")
    wait(ve, "vp4")
    inc(ve.tensor_copy(T.pl[:], T.pe16[:]), "vp5")
    wait(ve, "dlist")
    inc(ve.tensor_copy(T.pmo2[:], T.pmi2[:]), "vp2")
    inc(ve.tensor_copy(T.eno2[:], T.eni2[:]), "vp2")
    wait(ve, "pe0")
    inc(ve.tensor_copy(T.enc[:], T.psT[:, 0:128]), "venc")
    wait(ve, "arrM", "vown")
    inc(ve.tensor_tensor(T.t64[:], T.land[:, 0:64], T.land[:, 64:128], A.min), "vt1")
    wait(ve, "vt1")
    inc(ve.tensor_tensor(T.t32[:], T.t64[:, 0:32], T.t64[:, 32:64], A.min), "vt2")
    wait(ve, "vt2", "vrd0")
    inc(ve.tensor_tensor(T.red[:, 15:256:16], T.t32[:, 0:16], T.t32[:, 16:32], A.min), "vred")

    for h in (2, 3, 4):
        wait(ve, "vred", "vp5")
        inc(ve.tensor_copy(T.per[:, 0:96], T.red[:].indirect(T.pl[:, 0:6])), "vper")
        wait(se, "vred", "vp5")
        inc(se.activation(T.per[:, 96:144], T.red[:].indirect(T.pl[:, 6:9]), F.Copy), "sper")
        wait(pe, "vper", "sper", "gident")
        for name, b0, k in BANKS:
            for j in range(k):
                b = b0 + j
                inc(pe.transpose(T["ps" + name][:, 128 * j:128 * j + 128], T.per[:, 2 * b:2 * b + 128], T.ident[:]),
                    "pw" + name)
        for name, b0, k in BANKS:
            src, lo, hi = T["ps" + name][:, 0:128 * k], 128 * b0, 128 * (b0 + k)
            for half in (0, 1):
                dst = T.win[:, 1024 * half + lo:1024 * half + hi]
                if name in "ACE":
                    wait(ve, "pw" + name, "vbig")
                    inc(ve.tensor_scalar(dst, src, T.bigb[:, half:half + 1], None, A.max), "wv")
                else:
                    wait(se, "pw" + name, "vbig")
                    inc(se.activation(dst, src, F.Identity, bias=T.big[:, half:half + 1],
                                      scale=T.hal[:, half:half + 1]), "ws")
        phase(False, T.pmo2, T.eno2, T.stm2, ("wv", "ws", "vp2"), lambda b: T.psX[:, 16 * b:16 * b + 16], T.sel2[:])
        wait(ve, "px", "vmsk")
        inc(ve.tensor_tensor_scan(T.red[:], T.msk[:], T.psX[:, 0:256], 1.0, A.max, A.min), "vred")

    wait(ve, "vred")
    inc(ve.tensor_copy(T.ys[:], T.red[:, 15:256:16]), "vys")
    wait(g, "vys")
    send(lambda r: T.ys[:], T.land2[:, mine], "arrY")
    wait(ve, "vys")
    inc(ve.tensor_copy(T.land2[:, mine], T.ys[:]), "vown2")
    wait(pe, "arrY", "vown2")
    inc(pe.matmul(T.psT[:, 0:128], T.land2[:], T.ident[:], True, True), "pt")
    wait(ve, "arrY", "vown2", "venc")
    inc(ve.tensor_tensor(T.flg[:], T.land2[:], T.enc[:], A.is_equal), "vflg")
    wait(se, "pt")
    inc(se.activation(T.lnv[:], T.psT[:, 0:128], F.Ln, scale=2.0 ** 32), "sln")
    wait(ve, "sln", "sac")
    inc(ve.tensor_scalar(T.yi[:], T.lnv[:], T.acol[:, 0:1], 1024.0, A.mult, A.add), "vyi")
    wait(ve, "vyi")
    inc(ve.tensor_copy(T.yf[:], T.yi[:]), "vyf")
    wait(sy, "vyf")
    inc(sy.dma_start(T.y[:], T.yf[:]), "dy", 16)
    wait(pe, "vflg", "vones")
    for b in range(16):
        pc = pe.matmul(T.psR[0:8, 0:1], T.flg[:, b:128:16], T.ones[:, 0:1], b == 0, b == 15)
    inc(pc, "pc")
    wait(se, "pc")
    inc(se.activation(T.cf[0:8, 0:1], T.psR[0:8, 0:1], F.Copy), "scf")
    wait(se, "scf")
    inc(se.dma_start(T.cnt[:], T.cf[0:8, 0:1]), "dcnt", 16)
    wait(sy, "dy")
    wait(se, "dcnt")
    wait(g, "loc")
